import numpy as np
import ml_dtypes


def mxq(x, axis, fmt="e4m3"):
    dtype, down = {"e4m3": (ml_dtypes.float8_e4m3fn, 7), "e5m2": (ml_dtypes.float8_e5m2, 14)}[fmt]
    v = np.moveaxis(np.asarray(x, np.float32).astype(ml_dtypes.bfloat16).astype(np.float64), axis, -1)
    blocks = v.reshape(v.shape[:-1] + (-1, 32))
    amax = np.abs(blocks).max(-1, keepdims=True)
    byte = np.maximum(np.where(amax > 0, np.frexp(amax)[1] - 1 + 127, 0) - down, 1)
    scale = np.exp2(byte - 127.0)
    codes = (blocks / scale).astype(np.float32).astype(dtype).astype(np.float64)
    return np.moveaxis((codes * scale).reshape(v.shape), -1, axis)


WIDE = False


def mx_kscale(k):
    if not WIDE:
        return np.ones(k)
    levels = np.array([10, -10, 5, -5, 0])
    if k % 512:
        return np.exp2(np.random.permutation(np.resize(levels, k // 32))).repeat(32)
    a = np.empty((k // 512, 16))
    for p in range(k // 512):
        a[p, :8] = np.random.permutation(np.resize(levels, 8))
        for g in range(8):
            far = levels[np.abs(levels - a[p, g]) >= 10]
            a[p, g + 8] = far[np.random.randint(len(far))]
    return np.exp2(a.ravel()).repeat(32)


def f64(x):
    return np.asarray(x).astype(np.float64)


def striped(idx):
    return np.tile(idx.reshape(-1, 16).T, (8, 1)).astype(np.uint16)


def unstriped(offs):
    return offs[:16].T.reshape(-1).astype(np.int64)


def relu2(v):
    return np.maximum(v, 0.0) ** 2


K, T, E, C, N = 1536, 768, 12, 128, 128


def by_expert(wq, xq):
    return np.concatenate([wq[e].T @ xq[:, e * C:(e + 1) * C] for e in range(E)], axis=1)


def setup_inputs():
    n = np.random.standard_normal
    s = mx_kscale(K)[:, None]
    first = np.random.permutation(np.repeat(np.arange(E), T // E))
    second = (first + 1 + np.random.permutation(np.repeat(np.arange(E - 1), -(-T // (E - 1)))[:T])) % E
    while np.bincount(second, minlength=E).max() != T // E:
        load = np.bincount(second, minlength=E); hi, lo = int(load.argmax()), int(load.argmin())
        t = np.flatnonzero((second == hi) & (first != lo))[0]; second[t] = lo
    slot_token = np.empty(E * C, np.int64); pos = np.empty((2, T), np.int64); fill = np.zeros(E, np.int64)
    place = np.stack([np.random.permutation(C) for _ in range(E)])
    for r, deal in enumerate((first, second)):
        for t in np.random.permutation(T):
            e = deal[t]; j = e * C + place[e, fill[e]]; fill[e] += 1; slot_token[j] = t; pos[r, t] = j
    g = np.random.uniform(0.2, 0.8, T)
    w_slot = np.empty(E * C); w_slot[pos[0]] = g; w_slot[pos[1]] = 1.0 - g
    return {
        "xT": (n((K, T)) * s).astype(np.float32),
        "w": (n((E, K, N)) / np.sqrt(K) / s[None]).astype(np.float32),
        "b": (0.3 * n((N, E))).astype(np.float32),
        "gate": np.tile(w_slot, (K, 1)).astype(np.float32),
        "offs": striped(slot_token),
        "pos1": striped(pos[0]),
        "pos2": striped(pos[1]),
    }


def reference(xT, w, b, gate, offs, pos1, pos2):
    idx = unstriped(offs)
    xq = mxq(f64(gate) * f64(xT)[:, idx], 0, "e4m3")
    y = by_expert(mxq(f64(w), 1, "e4m3"), xq)
    y = relu2(y + np.repeat(f64(b), C, axis=1))
    return y[:, unstriped(pos1)] + y[:, unstriped(pos2)]

@@ -1,0 +1,187 @@
+from contextlib import ExitStack
+
+import concourse.mybir as mybir
+
+K, T, E, C, N = 1536, 768, 12, 128, 128
+S = E * C
+
+FLOPS = 2 * K * N * S
+BYTES = 4 * (K * T + E * K * N + N * E + S + N * T) + 2 * 128 * (S + 2 * T) // 16
+
+F32 = mybir.dt.float32
+BF16 = mybir.dt.bfloat16
+U32 = mybir.dt.uint32
+U16 = mybir.dt.uint16
+U8 = mybir.dt.uint8
+FP8X4 = mybir.dt.float8_e4m3fn_x4
+MULT = mybir.AluOpType.mult
+ADD = mybir.AluOpType.add
+RELU = mybir.ActivationFunctionType.Relu
+SQUARE = mybir.ActivationFunctionType.Square
+
+P = 128
+PACK = 4
+K_PASS = P * PACK
+PASSES = K // K_PASS
+GROUP = 4
+GROUPS = E // GROUP
+G_SLOTS = GROUP * C
+RUN = 4
+PER_COL = 16
+
+
+def tile_moe_pre_lin_relu2_kernel(tc, xT, w, b, gate, offs, pos1, pos2, out):
+    nc = tc.nc
+    with ExitStack() as ctx:
+        keep = ctx.enter_context(tc.tile_pool(name="keep", bufs=1))
+        ring = ctx.enter_context(tc.tile_pool(name="ring", bufs=2))
+        psum = ctx.enter_context(tc.psum_pool(name="psum", bufs=1))
+
+        offs_sb = keep.tile([P, S // PER_COL], U16, name="offs_sb")
+        pos1_sb = keep.tile([P, T // PER_COL], U16, name="pos1_sb")
+        pos2_sb = keep.tile([P, T // PER_COL], U16, name="pos2_sb")
+        b_sb = keep.tile([P, E], F32, name="b_sb")
+        x_sb = {(g, j): keep.tile([P, T], F32, name=f"x_{g}_{j}") for g in range(PASSES) for j in range(PACK)}
+        gate_sb = [keep.tile([P, G_SLOTS], F32, name=f"gate_{s}") for s in range(GROUPS)]
+        w_sb = {(g, s): keep.tile([P, GROUP, PACK * N], F32, name=f"w_{g}_{s}") for g in range(PASSES) for s in range(GROUPS)}
+        y = keep.tile([P, S], F32, name="y")
+
+        def load_x(g, j):
+            rows = xT[g * K_PASS : (g + 1) * K_PASS, :].rearrange("(p j) t -> p j t", j=PACK)
+            nc.sync.dma_start(out=x_sb[g, j][:], in_=rows[:, j, :])
+
+        def load_gate(s):
+            nc.sync.dma_start(out=gate_sb[s][:], in_=gate[0:P, s * G_SLOTS : (s + 1) * G_SLOTS])
+
+        def load_w(g, s):
+            src = w[s * GROUP : (s + 1) * GROUP, g * K_PASS : (g + 1) * K_PASS, :]
+            nc.sync.dma_start(out=w_sb[g, s][:], in_=src.rearrange("e (p j) n -> p e (j n)", j=PACK))
+
+        order = [(g, s) for g in range(PASSES) for s in range(GROUPS - 1)] + [(g, GROUPS - 1) for g in range(PASSES)]
+
+        nc.sync.dma_start(offs_sb[:], offs)
+        load_x(0, 0)
+        load_gate(0)
+        for j in range(1, PACK):
+            load_x(0, j)
+        load_gate(1)
+        load_w(*order[0])
+        for j in range(PACK):
+            load_x(1, j)
+        load_w(*order[1])
+        load_w(*order[2])
+        for j in range(PACK):
+            load_x(2, j)
+        load_w(*order[3])
+        load_w(*order[4])
+        nc.sync.dma_start(out=b_sb[:], in_=b)
+        load_w(*order[5])
+        load_gate(2)
+        for u in range(6, 9):
+            load_w(*order[u])
+        nc.sync.dma_start(pos1_sb[:], pos1)
+        nc.sync.dma_start(pos2_sb[:], pos2)
+
+        x_codes, x_scales, w_codes, w_scales = {}, {}, {}, {}
+
+        def gather(g, e0, n_e):
+            width = n_e * C
+            picked = ring.tile([P, PACK, width], F32, name="picked")
+            s, c0 = divmod(e0 * C, G_SLOTS)
+            lst = offs_sb[:, e0 * C // PER_COL : (e0 * C + width) // PER_COL]
+            for j in range(PACK):
+                nc.vector.tensor_tensor(picked[:, j, :], x_sb[g, j][:].indirect(lst), gate_sb[s][:, c0 : c0 + width], MULT)
+            return picked
+
+        def round_x(picked, n_e):
+            width = n_e * C
+            grouped = ring.tile([P, width, PACK], BF16, name="x_grouped", align_bytes=64)
+            nc.scalar.copy(
+                out=grouped[:].rearrange("p (c i) j -> p c j i", i=RUN),
+                in_=picked[:].rearrange("p j (c i) -> p c j i", i=RUN),
+            )
+            return grouped
+
+        def quantize(grouped, width, name):
+            codes = keep.tile([P, width], U32, name=f"{name}_codes", align_bytes=64)
+            scales = keep.tile([P, width], U8, name=f"{name}_scales", align_bytes=64)
+            nc.vector.quantize_mx(out=codes[:].bitcast(FP8X4), scales=scales[:], in_=grouped[:].rearrange("p c j -> p (c j)"))
+            return codes, scales
+
+        def quantize_x(grouped, g, e0, n_e):
+            codes, scales = quantize(grouped, n_e * C, f"x_{g}_{e0}")
+            for i in range(n_e):
+                x_codes[g, e0 + i] = codes[:, i * C : (i + 1) * C]
+                x_scales[g, e0 + i] = scales[:, i * C : (i + 1) * C]
+
+        def prepare_w(g, s):
+            grouped = ring.tile([P, GROUP * N, PACK], BF16, name="w_grouped", align_bytes=64)
+            nc.scalar.copy(
+                out=grouped[:].rearrange("p (e c i) j -> p e c j i", e=GROUP, i=RUN),
+                in_=w_sb[g, s][:].rearrange("p e (j c i) -> p e c j i", j=PACK, i=RUN),
+            )
+            codes, scales = quantize(grouped, GROUP * N, f"w_{g}_{s}")
+            for i in range(GROUP):
+                w_codes[g, s * GROUP + i] = codes[:, i * N : (i + 1) * N]
+                w_scales[g, s * GROUP + i] = scales[:, i * N : (i + 1) * N]
+
+        def product(acc, g, e):
+            nc.tensor.matmul_mx(
+                out=acc,
+                lhsT=w_codes[g, e].bitcast(FP8X4),
+                lhsT_scale=w_scales[g, e],
+                rhs=x_codes[g, e].bitcast(FP8X4),
+                rhs_scale=x_scales[g, e],
+                start=(g == 0),
+                stop=(g == PASSES - 1),
+            )
+
+        def finish(accs, e0):
+            relu = ring.tile([P, len(accs) * C], F32, name="relu")
+            for i, acc in enumerate(accs):
+                e = e0 + i
+                nc.scalar.activation(out=relu[:, i * C : (i + 1) * C], in_=acc, func=RELU, bias=b_sb[:, e : e + 1])
+            nc.scalar.activation(out=y[:, e0 * C : (e0 + len(accs)) * C], in_=relu[:], func=SQUARE)
+
+        def whole_group(s):
+            bank = psum.tile([P, G_SLOTS], F32, name=f"bank_{s}")
+            accs = [bank[:, i * C : (i + 1) * C] for i in range(GROUP)]
+            for i in range(GROUP):
+                for g in range(PASSES):
+                    product(accs[i], g, s * GROUP + i)
+            finish(accs, s * GROUP)
+
+        last_e0 = (GROUPS - 1) * GROUP
+        last_acc = [psum.tile([P, C], F32, name=f"last_{i}") for i in range(GROUP)]
+
+        steps = [(g, s * GROUP, GROUP) for g, s in order[:-1]]
+        steps = steps + [(PASSES - 1, last_e0, 2), (PASSES - 1, last_e0 + 2, 1), (PASSES - 1, last_e0 + 3, 1)]
+        w_after = {0: [0], 1: [1], 2: [2, 3], 3: [4], 4: [5, 6], 5: [7], 6: [8]}
+
+        picked = gather(*steps[0])
+        for u, (g, e0, n_e) in enumerate(steps):
+            following = gather(*steps[u + 1]) if u + 1 < len(steps) else None
+            grouped = round_x(picked, n_e)
+            quantize_x(grouped, g, e0, n_e)
+            for v in w_after.get(u, []):
+                prepare_w(*order[v])
+            if e0 < last_e0:
+                if g == PASSES - 1:
+                    whole_group(e0 // GROUP)
+            else:
+                for e in range(e0, e0 + n_e):
+                    product(last_acc[e - last_e0][:], g, e)
+                if g == PASSES - 1:
+                    finish([last_acc[e - last_e0][:] for e in range(e0, e0 + n_e)], e0)
+            picked = following
+
+        halves = 2
+        half = T // halves
+        cols = half // PER_COL
+        first = [keep.tile([P, half], F32, name=f"first_{h}") for h in range(halves)]
+        total = [keep.tile([P, half], F32, name=f"total_{h}") for h in range(halves)]
+        for h in range(halves):
+            nc.vector.tensor_copy(first[h][:], y[:].indirect(pos1_sb[:, h * cols : (h + 1) * cols]))
+        for h in range(halves):
+            nc.vector.tensor_tensor(total[h][:], y[:].indirect(pos2_sb[:, h * cols : (h + 1) * cols]), first[h][:], ADD)
+            nc.sync.dma_start(out=out[:, h * half : (h + 1) * half], in_=total[h][:])

@@ -28,6 +28,9 @@ GROUPS = E // GROUP
 G_SLOTS = GROUP * C
 RUN = 4
 PER_COL = 16
+WIDE = 2 * G_SLOTS
+WINDOW = WIDE + PER_COL
+GATE_FIRST = 256
 
 
 def tile_moe_pre_lin_relu2_kernel(tc, xT, w, b, gate, offs, pos1, pos2, out):
@@ -41,17 +44,17 @@ def tile_moe_pre_lin_relu2_kernel(tc, xT, w, b, gate, offs, pos1, pos2, out):
         pos1_sb = keep.tile([P, T // PER_COL], U16, name="pos1_sb")
         pos2_sb = keep.tile([P, T // PER_COL], U16, name="pos2_sb")
         b_sb = keep.tile([P, E], F32, name="b_sb")
-        x_sb = {(g, j): keep.tile([P, T], F32, name=f"x_{g}_{j}") for g in range(PASSES) for j in range(PACK)}
-        gate_sb = [keep.tile([P, G_SLOTS], F32, name=f"gate_{s}") for s in range(GROUPS)]
-        w_sb = {(g, s): keep.tile([P, GROUP, PACK * N], F32, name=f"w_{g}_{s}") for g in range(PASSES) for s in range(GROUPS)}
+        x_sb = {(g, j): keep.tile([P, WINDOW], F32, name=f"x_{g}_{j}") for g in range(PASSES) for j in range(PACK)}
+        gate_sb = keep.tile([P, S], F32, name="gate_sb")
+        w_sb = {(g, s): keep.tile([P, GROUP, PACK * N], F32, name=f"w_{g}_{s}", tag=f"stage_{g}_{s}", align_bytes=64) for g in range(PASSES) for s in range(GROUPS)}
         y = keep.tile([P, S], F32, name="y")
 
         def load_x(g, j):
             rows = xT[g * K_PASS : (g + 1) * K_PASS, :].rearrange("(p j) t -> p j t", j=PACK)
-            nc.sync.dma_start(out=x_sb[g, j][:], in_=rows[:, j, :])
+            nc.sync.dma_start(out=x_sb[g, j][:, 0:T], in_=rows[:, j, :])
 
-        def load_gate(s):
-            nc.sync.dma_start(out=gate_sb[s][:], in_=gate[0:P, s * G_SLOTS : (s + 1) * G_SLOTS])
+        def load_gate(c0, c1):
+            nc.sync.dma_start(out=gate_sb[:, c0:c1], in_=gate[0:P, c0:c1])
 
         def load_w(g, s):
             src = w[s * GROUP : (s + 1) * GROUP, g * K_PASS : (g + 1) * K_PASS, :]
@@ -59,24 +62,33 @@ def tile_moe_pre_lin_relu2_kernel(tc, xT, w, b, gate, offs, pos1, pos2, out):
 
         order = [(g, s) for g in range(PASSES) for s in range(GROUPS - 1)] + [(g, GROUPS - 1) for g in range(PASSES)]
 
+        for g in range(PASSES):
+            for j in range(PACK):
+                nc.gpsimd.memset(x_sb[g, j][:, T:WINDOW], 0.0)
+
         nc.sync.dma_start(offs_sb[:], offs)
         load_x(0, 0)
-        load_gate(0)
-        for j in range(1, PACK):
-            load_x(0, j)
-        load_gate(1)
+        load_gate(0, GATE_FIRST)
+        load_gate(GATE_FIRST, WIDE)
+        load_x(0, 1)
+        load_x(0, 2)
         load_w(*order[0])
-        for j in range(PACK):
-            load_x(1, j)
+        load_x(0, 3)
+        load_x(1, 0)
         load_w(*order[1])
+        load_x(1, 1)
+        load_x(1, 2)
         load_w(*order[2])
-        for j in range(PACK):
-            load_x(2, j)
+        load_x(1, 3)
         load_w(*order[3])
+        load_x(2, 0)
+        load_x(2, 1)
         load_w(*order[4])
-        nc.sync.dma_start(out=b_sb[:], in_=b)
+        load_x(2, 2)
+        load_x(2, 3)
         load_w(*order[5])
-        load_gate(2)
+        load_gate(WIDE, S)
+        nc.sync.dma_start(out=b_sb[:], in_=b)
         for u in range(6, 9):
             load_w(*order[u])
         nc.sync.dma_start(pos1_sb[:], pos1)
@@ -86,17 +98,19 @@ def tile_moe_pre_lin_relu2_kernel(tc, xT, w, b, gate, offs, pos1, pos2, out):
 
         def gather(g, e0, n_e):
             width = n_e * C
+            first = e0 * C
             picked = ring.tile([P, PACK, width], F32, name="picked")
-            s, c0 = divmod(e0 * C, G_SLOTS)
-            lst = offs_sb[:, e0 * C // PER_COL : (e0 * C + width) // PER_COL]
             for j in range(PACK):
-                nc.vector.tensor_tensor(picked[:, j, :], x_sb[g, j][:].indirect(lst), gate_sb[s][:, c0 : c0 + width], MULT)
+                cuts = [0, GATE_FIRST, width] if (g, e0, j) == (0, 0, 0) else [0, width]
+                for c0, c1 in zip(cuts, cuts[1:]):
+                    lst = offs_sb[:, (first + c0) // PER_COL : (first + c1) // PER_COL]
+                    nc.vector.tensor_tensor(picked[:, j, c0:c1], x_sb[g, j][:].indirect(lst), gate_sb[:, first + c0 : first + c1], MULT)
             return picked
 
-        def round_x(picked, n_e):
+        def round_x(picked, n_e, tag, copy):
             width = n_e * C
-            grouped = ring.tile([P, width, PACK], BF16, name="x_grouped", align_bytes=64)
-            nc.scalar.copy(
+            grouped = keep.tile([P, width, PACK], BF16, name="x_grouped", tag=tag, align_bytes=64)
+            copy(
                 out=grouped[:].rearrange("p (c i) j -> p c j i", i=RUN),
                 in_=picked[:].rearrange("p j (c i) -> p c j i", i=RUN),
             )
@@ -115,7 +129,7 @@ def tile_moe_pre_lin_relu2_kernel(tc, xT, w, b, gate, offs, pos1, pos2, out):
                 x_scales[g, e0 + i] = scales[:, i * C : (i + 1) * C]
 
         def prepare_w(g, s):
-            grouped = ring.tile([P, GROUP * N, PACK], BF16, name="w_grouped", align_bytes=64)
+            grouped = ring.tile([P, GROUP * N, PACK], BF16, name="w_grouped", align_bytes=64, bufs=3)
             nc.scalar.copy(
                 out=grouped[:].rearrange("p (e c i) j -> p e c j i", e=GROUP, i=RUN),
                 in_=w_sb[g, s][:].rearrange("p e (j c i) -> p e c j i", j=PACK, i=RUN),
@@ -154,34 +168,36 @@ def tile_moe_pre_lin_relu2_kernel(tc, xT, w, b, gate, offs, pos1, pos2, out):
         last_e0 = (GROUPS - 1) * GROUP
         last_acc = [psum.tile([P, C], F32, name=f"last_{i}") for i in range(GROUP)]
 
-        steps = [(g, s * GROUP, GROUP) for g, s in order[:-1]]
+        steps = [(g, 0, 2 * GROUP) for g in range(PASSES)] + [(g, last_e0, GROUP) for g in range(PASSES - 1)]
         steps = steps + [(PASSES - 1, last_e0, 2), (PASSES - 1, last_e0 + 2, 1), (PASSES - 1, last_e0 + 3, 1)]
-        w_after = {0: [0], 1: [1], 2: [2, 3], 3: [4], 4: [5, 6], 5: [7], 6: [8]}
+        w_before = {0: [0, 1], 1: [2, 3], 2: [4, 5, 6], 3: [7], 4: [8]}
 
         picked = gather(*steps[0])
         for u, (g, e0, n_e) in enumerate(steps):
             following = gather(*steps[u + 1]) if u + 1 < len(steps) else None
-            grouped = round_x(picked, n_e)
-            quantize_x(grouped, g, e0, n_e)
-            for v in w_after.get(u, []):
+            for v in w_before.get(u, []):
                 prepare_w(*order[v])
-            if e0 < last_e0:
-                if g == PASSES - 1:
-                    whole_group(e0 // GROUP)
-            else:
+            tag = "stage_%d_%d" % order[w_before[u][-1]] if u in w_before else f"x_small_{u}"
+            grouped = round_x(picked, n_e, tag, nc.vector.tensor_copy if following is None else nc.scalar.copy)
+            quantize_x(grouped, g, e0, n_e)
+            if e0 == last_e0 and n_e == GROUP:
                 for e in range(e0, e0 + n_e):
                     product(last_acc[e - last_e0][:], g, e)
-                if g == PASSES - 1:
-                    finish([last_acc[e - last_e0][:] for e in range(e0, e0 + n_e)], e0)
+                if g == PASSES - 2:
+                    whole_group(0)
+            elif e0 >= last_e0:
+                if e0 == last_e0:
+                    whole_group(1)
+                for e in range(e0, e0 + n_e):
+                    product(last_acc[e - last_e0][:], g, e)
+                finish([last_acc[e - last_e0][:] for e in range(e0, e0 + n_e)], e0)
             picked = following
 
-        halves = 2
-        half = T // halves
-        cols = half // PER_COL
-        first = [keep.tile([P, half], F32, name=f"first_{h}") for h in range(halves)]
-        total = [keep.tile([P, half], F32, name=f"total_{h}") for h in range(halves)]
-        for h in range(halves):
-            nc.vector.tensor_copy(first[h][:], y[:].indirect(pos1_sb[:, h * cols : (h + 1) * cols]))
-        for h in range(halves):
-            nc.vector.tensor_tensor(total[h][:], y[:].indirect(pos2_sb[:, h * cols : (h + 1) * cols]), first[h][:], ADD)
-            nc.sync.dma_start(out=out[:, h * half : (h + 1) * half], in_=total[h][:])
+        parts = [(0, 512), (512, T)]
+        first = [keep.tile([P, t1 - t0], F32, name=f"first_{t0}") for t0, t1 in parts]
+        total = [keep.tile([P, t1 - t0], F32, name=f"total_{t0}") for t0, t1 in parts]
+        for h, (t0, t1) in enumerate(parts):
+            nc.vector.tensor_copy(first[h][:], y[:].indirect(pos1_sb[:, t0 // PER_COL : t1 // PER_COL]))
+        for h, (t0, t1) in enumerate(parts):
+            nc.vector.tensor_tensor(total[h][:], y[:].indirect(pos2_sb[:, t0 // PER_COL : t1 // PER_COL]), first[h][:], ADD)
+            nc.sync.dma_start(out=out[:, t0:t1], in_=total[h][:])

@@ -16,6 +16,7 @@ U8 = mybir.dt.uint8
 FP8X4 = mybir.dt.float8_e4m3fn_x4
 MULT = mybir.AluOpType.mult
 ADD = mybir.AluOpType.add
+MAX = mybir.AluOpType.max
 RELU = mybir.ActivationFunctionType.Relu
 SQUARE = mybir.ActivationFunctionType.Square
 
@@ -23,14 +24,16 @@ P = 128
 PACK = 4
 K_PASS = P * PACK
 PASSES = K // K_PASS
-GROUP = 4
-GROUPS = E // GROUP
-G_SLOTS = GROUP * C
-RUN = 4
 PER_COL = 16
-WIDE = 2 * G_SLOTS
-WINDOW = WIDE + PER_COL
-GATE_FIRST = 256
+RUN = 4
+GROUP = 4
+PAIR = 2
+BANKS = 8
+EARLY = BANKS
+EARLY_SLOTS = EARLY * C
+WINDOW = EARLY_SLOTS + PER_COL
+GATE_FIRST = 320
+OUT_SPLIT = 512
 
 
 def tile_moe_pre_lin_relu2_kernel(tc, xT, w, b, gate, offs, pos1, pos2, out):
@@ -46,8 +49,17 @@ def tile_moe_pre_lin_relu2_kernel(tc, xT, w, b, gate, offs, pos1, pos2, out):
         b_sb = keep.tile([P, E], F32, name="b_sb")
         x_sb = {(g, j): keep.tile([P, WINDOW], F32, name=f"x_{g}_{j}") for g in range(PASSES) for j in range(PACK)}
         gate_sb = keep.tile([P, S], F32, name="gate_sb")
-        w_sb = {(g, s): keep.tile([P, GROUP, PACK * N], F32, name=f"w_{g}_{s}", tag=f"stage_{g}_{s}", align_bytes=64) for g in range(PASSES) for s in range(GROUPS)}
+        w_sb = {
+            (g, e0): keep.tile([P, PAIR, PACK * N], F32, name=f"w_{g}_{e0}", tag=f"stage_{g}_{e0}", align_bytes=64)
+            for g in range(PASSES)
+            for e0 in range(0, E, PAIR)
+        }
         y = keep.tile([P, S], F32, name="y")
+
+        late = E - EARLY
+        steps = [(g, 0, EARLY) for g in range(PASSES)] + [(g, EARLY, late) for g in range(PASSES - 1)]
+        steps = steps + [(PASSES - 1, EARLY, 2), (PASSES - 1, EARLY + 2, 1), (PASSES - 1, EARLY + 3, 1)]
+        w_groups = [(g, e0) for g in range(PASSES) for e0 in range(0, EARLY, GROUP)] + [(g, EARLY) for g in range(PASSES)]
 
         def load_x(g, j):
             rows = xT[g * K_PASS : (g + 1) * K_PASS, :].rearrange("(p j) t -> p j t", j=PACK)
@@ -56,144 +68,135 @@ def tile_moe_pre_lin_relu2_kernel(tc, xT, w, b, gate, offs, pos1, pos2, out):
         def load_gate(c0, c1):
             nc.sync.dma_start(out=gate_sb[:, c0:c1], in_=gate[0:P, c0:c1])
 
-        def load_w(g, s):
-            src = w[s * GROUP : (s + 1) * GROUP, g * K_PASS : (g + 1) * K_PASS, :]
-            nc.sync.dma_start(out=w_sb[g, s][:], in_=src.rearrange("e (p j) n -> p e (j n)", j=PACK))
+        def load_w(g, e0):
+            src = w[e0 : e0 + PAIR, g * K_PASS : (g + 1) * K_PASS, :]
+            nc.sync.dma_start(out=w_sb[g, e0][:], in_=src.rearrange("e (p j) n -> p e (j n)", j=PACK))
 
-        order = [(g, s) for g in range(PASSES) for s in range(GROUPS - 1)] + [(g, GROUPS - 1) for g in range(PASSES)]
-
-        for g in range(PASSES):
-            for j in range(PACK):
-                nc.gpsimd.memset(x_sb[g, j][:, T:WINDOW], 0.0)
+        for window in x_sb.values():
+            nc.gpsimd.memset(window[:, T:WINDOW], 0.0)
 
         nc.sync.dma_start(offs_sb[:], offs)
         load_x(0, 0)
         load_gate(0, GATE_FIRST)
-        load_gate(GATE_FIRST, WIDE)
-        load_x(0, 1)
-        load_x(0, 2)
-        load_w(*order[0])
-        load_x(0, 3)
-        load_x(1, 0)
-        load_w(*order[1])
-        load_x(1, 1)
-        load_x(1, 2)
-        load_w(*order[2])
-        load_x(1, 3)
-        load_w(*order[3])
-        load_x(2, 0)
-        load_x(2, 1)
-        load_w(*order[4])
-        load_x(2, 2)
-        load_x(2, 3)
-        load_w(*order[5])
-        load_gate(WIDE, S)
+        load_gate(GATE_FIRST, EARLY_SLOTS)
+        w_pairs = [(g, e0 + i) for g, e0 in w_groups for i in range(0, GROUP, PAIR)]
+        later_x = list(x_sb)[1:]
+        for window, pair in zip(later_x, w_pairs):
+            load_x(*window)
+            load_w(*pair)
+        load_gate(EARLY_SLOTS, S)
         nc.sync.dma_start(out=b_sb[:], in_=b)
-        for u in range(6, 9):
-            load_w(*order[u])
+        for pair in w_pairs[len(later_x) :]:
+            load_w(*pair)
         nc.sync.dma_start(pos1_sb[:], pos1)
         nc.sync.dma_start(pos2_sb[:], pos2)
 
-        x_codes, x_scales, w_codes, w_scales = {}, {}, {}, {}
+        x_codes, x_scales, w_codes, w_scales, acc = {}, {}, {}, {}, {}
 
         def gather(g, e0, n_e):
             width = n_e * C
-            first = e0 * C
+            slot0 = e0 * C
             picked = ring.tile([P, PACK, width], F32, name="picked")
             for j in range(PACK):
                 cuts = [0, GATE_FIRST, width] if (g, e0, j) == (0, 0, 0) else [0, width]
                 for c0, c1 in zip(cuts, cuts[1:]):
-                    lst = offs_sb[:, (first + c0) // PER_COL : (first + c1) // PER_COL]
-                    nc.vector.tensor_tensor(picked[:, j, c0:c1], x_sb[g, j][:].indirect(lst), gate_sb[:, first + c0 : first + c1], MULT)
+                    entries = offs_sb[:, (slot0 + c0) // PER_COL : (slot0 + c1) // PER_COL]
+                    window = x_sb[g, j][:].indirect(entries)
+                    nc.vector.tensor_tensor(picked[:, j, c0:c1], window, gate_sb[:, slot0 + c0 : slot0 + c1], MULT)
             return picked
 
-        def round_x(picked, n_e, tag, copy):
-            width = n_e * C
-            grouped = keep.tile([P, width, PACK], BF16, name="x_grouped", tag=tag, align_bytes=64)
-            copy(
-                out=grouped[:].rearrange("p (c i) j -> p c j i", i=RUN),
-                in_=picked[:].rearrange("p j (c i) -> p c j i", i=RUN),
-            )
-            return grouped
+        spent = []
 
-        def quantize(grouped, width, name):
+        def bf16_tile(name, width, place):
+            tag = spent.pop(place) if spent else name
+            return keep.tile([P, width, PACK], BF16, name=name, tag=tag, align_bytes=64)
+
+        def quantize(grouped, name):
+            width = grouped.shape[1]
             codes = keep.tile([P, width], U32, name=f"{name}_codes", align_bytes=64)
             scales = keep.tile([P, width], U8, name=f"{name}_scales", align_bytes=64)
             nc.vector.quantize_mx(out=codes[:].bitcast(FP8X4), scales=scales[:], in_=grouped[:].rearrange("p c j -> p (c j)"))
             return codes, scales
 
-        def quantize_x(grouped, g, e0, n_e):
-            codes, scales = quantize(grouped, n_e * C, f"x_{g}_{e0}")
+        def prepare_x(picked, g, e0, n_e, place, copy):
+            grouped = bf16_tile("x_grouped", n_e * C, place)
+            copy(
+                out=grouped[:].rearrange("p (c i) j -> p c j i", i=RUN),
+                in_=picked[:].rearrange("p j (c i) -> p c j i", i=RUN),
+            )
+            codes, scales = quantize(grouped, f"x_{g}_{e0}")
             for i in range(n_e):
                 x_codes[g, e0 + i] = codes[:, i * C : (i + 1) * C]
                 x_scales[g, e0 + i] = scales[:, i * C : (i + 1) * C]
 
-        def prepare_w(g, s):
-            grouped = ring.tile([P, GROUP * N, PACK], BF16, name="w_grouped", align_bytes=64, bufs=3)
-            nc.scalar.copy(
-                out=grouped[:].rearrange("p (e c i) j -> p e c j i", e=GROUP, i=RUN),
-                in_=w_sb[g, s][:].rearrange("p e (j c i) -> p e c j i", j=PACK, i=RUN),
-            )
-            codes, scales = quantize(grouped, GROUP * N, f"w_{g}_{s}")
+        def prepare_w(g, e0):
+            grouped = bf16_tile(f"w_grouped_{g}_{e0}", GROUP * N, 0)
+            for i in range(0, GROUP, PAIR):
+                nc.scalar.copy(
+                    out=grouped[:, i * N : (i + PAIR) * N, :].rearrange("p (e c i) j -> p e c j i", e=PAIR, i=RUN),
+                    in_=w_sb[g, e0 + i][:].rearrange("p e (j c i) -> p e c j i", j=PACK, i=RUN),
+                )
+                spent.append(f"stage_{g}_{e0 + i}")
+            codes, scales = quantize(grouped, f"w_{g}_{e0}")
             for i in range(GROUP):
-                w_codes[g, s * GROUP + i] = codes[:, i * N : (i + 1) * N]
-                w_scales[g, s * GROUP + i] = scales[:, i * N : (i + 1) * N]
+                w_codes[g, e0 + i] = codes[:, i * N : (i + 1) * N]
+                w_scales[g, e0 + i] = scales[:, i * N : (i + 1) * N]
 
-        def product(acc, g, e):
-            nc.tensor.matmul_mx(
-                out=acc,
-                lhsT=w_codes[g, e].bitcast(FP8X4),
-                lhsT_scale=w_scales[g, e],
-                rhs=x_codes[g, e].bitcast(FP8X4),
-                rhs_scale=x_scales[g, e],
-                start=(g == 0),
-                stop=(g == PASSES - 1),
-            )
+        def multiply(g, e0, n_e):
+            for e in range(e0, e0 + n_e):
+                if g == 0:
+                    acc[e] = psum.tile([P, C], F32, name="acc", tag=f"bank_{e % BANKS}")
+                nc.tensor.matmul_mx(
+                    out=acc[e][:],
+                    lhsT=w_codes[g, e].bitcast(FP8X4),
+                    lhsT_scale=w_scales[g, e],
+                    rhs=x_codes[g, e].bitcast(FP8X4),
+                    rhs_scale=x_scales[g, e],
+                    start=(g == 0),
+                    stop=(g == PASSES - 1),
+                )
 
-        def finish(accs, e0):
-            relu = ring.tile([P, len(accs) * C], F32, name="relu")
-            for i, acc in enumerate(accs):
+        def finish(e0, n_e):
+            relu = ring.tile([P, n_e * C], F32, name="relu")
+            for i in range(n_e):
                 e = e0 + i
-                nc.scalar.activation(out=relu[:, i * C : (i + 1) * C], in_=acc, func=RELU, bias=b_sb[:, e : e + 1])
-            nc.scalar.activation(out=y[:, e0 * C : (e0 + len(accs)) * C], in_=relu[:], func=SQUARE)
+                nc.scalar.activation(out=relu[:, i * C : (i + 1) * C], in_=acc[e][:], func=RELU, bias=b_sb[:, e : e + 1])
+            nc.scalar.activation(out=y[:, e0 * C : (e0 + n_e) * C], in_=relu[:], func=SQUARE)
 
-        def whole_group(s):
-            bank = psum.tile([P, G_SLOTS], F32, name=f"bank_{s}")
-            accs = [bank[:, i * C : (i + 1) * C] for i in range(GROUP)]
-            for i in range(GROUP):
-                for g in range(PASSES):
-                    product(accs[i], g, s * GROUP + i)
-            finish(accs, s * GROUP)
+        def finish_on_vector(e):
+            relu = keep.tile([P, C], F32, name="relu_last")
+            nc.vector.tensor_scalar(out=relu[:], in0=acc[e][:], scalar1=b_sb[:, e : e + 1], scalar2=0.0, op0=ADD, op1=MAX)
+            nc.vector.tensor_tensor(y[:, e * C : (e + 1) * C], relu[:], relu[:], MULT)
 
-        last_e0 = (GROUPS - 1) * GROUP
-        last_acc = [psum.tile([P, C], F32, name=f"last_{i}") for i in range(GROUP)]
+        groups_before = [2, 2, 3, 0, 2, 0, 0, 0]
+        first_late = PASSES
 
-        steps = [(g, 0, 2 * GROUP) for g in range(PASSES)] + [(g, last_e0, GROUP) for g in range(PASSES - 1)]
-        steps = steps + [(PASSES - 1, last_e0, 2), (PASSES - 1, last_e0 + 2, 1), (PASSES - 1, last_e0 + 3, 1)]
-        w_before = {0: [0, 1], 1: [2, 3], 2: [4, 5, 6], 3: [7], 4: [8]}
-
+        done = 0
         picked = gather(*steps[0])
         for u, (g, e0, n_e) in enumerate(steps):
-            following = gather(*steps[u + 1]) if u + 1 < len(steps) else None
-            for v in w_before.get(u, []):
-                prepare_w(*order[v])
-            tag = "stage_%d_%d" % order[w_before[u][-1]] if u in w_before else f"x_small_{u}"
-            grouped = round_x(picked, n_e, tag, nc.vector.tensor_copy if following is None else nc.scalar.copy)
-            quantize_x(grouped, g, e0, n_e)
-            if e0 == last_e0 and n_e == GROUP:
-                for e in range(e0, e0 + n_e):
-                    product(last_acc[e - last_e0][:], g, e)
-                if g == PASSES - 2:
-                    whole_group(0)
-            elif e0 >= last_e0:
-                if e0 == last_e0:
-                    whole_group(1)
-                for e in range(e0, e0 + n_e):
-                    product(last_acc[e - last_e0][:], g, e)
-                finish([last_acc[e - last_e0][:] for e in range(e0, e0 + n_e)], e0)
+            last = u + 1 == len(steps)
+            following = None if last else gather(*steps[u + 1])
+            for group in w_groups[done : done + groups_before[u]]:
+                prepare_w(*group)
+            done = done + groups_before[u]
+            place = -1 if u in (0, first_late) else -2
+            prepare_x(picked, g, e0, n_e, place, nc.vector.tensor_copy if last else nc.scalar.copy)
+            if u < first_late:
+                multiply(g, e0, n_e)
+            elif g == 1:
+                finish(0, late)
+                multiply(0, e0, n_e)
+                multiply(1, e0, n_e)
+            elif g == PASSES - 1:
+                multiply(g, e0, n_e)
+                if u + 2 == len(steps):
+                    finish(late, EARLY - late)
+                    finish(EARLY, late - 1)
+                if last:
+                    finish_on_vector(e0)
             picked = following
 
-        parts = [(0, 512), (512, T)]
+        parts = [(0, OUT_SPLIT), (OUT_SPLIT, T)]
         first = [keep.tile([P, t1 - t0], F32, name=f"first_{t0}") for t0, t1 in parts]
         total = [keep.tile([P, t1 - t0], F32, name=f"total_{t0}") for t0, t1 in parts]
         for h, (t0, t1) in enumerate(parts):

@@ -1,6 +1,7 @@
 from contextlib import ExitStack
 
 import concourse.mybir as mybir
+from concourse.masks import make_identity
 
 K, T, E, C, N = 1536, 768, 12, 128, 128
 S = E * C
@@ -19,6 +20,7 @@ ADD = mybir.AluOpType.add
 MAX = mybir.AluOpType.max
 RELU = mybir.ActivationFunctionType.Relu
 SQUARE = mybir.ActivationFunctionType.Square
+COPY = mybir.ActivationFunctionType.Copy
 
 P = 128
 PACK = 4
@@ -32,7 +34,6 @@ BANKS = 8
 EARLY = BANKS
 EARLY_SLOTS = EARLY * C
 WINDOW = EARLY_SLOTS + PER_COL
-GATE_FIRST = 320
 OUT_SPLIT = 512
 
 
@@ -72,16 +73,22 @@ def tile_moe_pre_lin_relu2_kernel(tc, xT, w, b, gate, offs, pos1, pos2, out):
             src = w[e0 : e0 + PAIR, g * K_PASS : (g + 1) * K_PASS, :]
             nc.sync.dma_start(out=w_sb[g, e0][:], in_=src.rearrange("e (p j) n -> p e (j n)", j=PACK))
 
+        ident = keep.tile([P, P], F32, name="ident")
+        make_identity(nc, ident[:])
+        gate_col = keep.tile([P, EARLY], F32, name="gate_col")
         for window in x_sb.values():
             nc.gpsimd.memset(window[:, T:WINDOW], 0.0)
 
         nc.sync.dma_start(offs_sb[:], offs)
         load_x(0, 0)
-        load_gate(0, GATE_FIRST)
-        load_gate(GATE_FIRST, EARLY_SLOTS)
         w_pairs = [(g, e0 + i) for g, e0 in w_groups for i in range(0, GROUP, PAIR)]
         later_x = list(x_sb)[1:]
         for window, pair in zip(later_x, w_pairs):
+            if window == (0, 2):
+                with nc.allow_non_contiguous_dma(reason="one gate value a partition"):
+                    nc.sync.dma_start(out=gate_col[:], in_=gate[0, 0:EARLY_SLOTS].rearrange("(e p) -> p e", p=P))
+            if window == (1, 0):
+                load_gate(0, EARLY_SLOTS)
             load_x(*window)
             load_w(*pair)
         load_gate(EARLY_SLOTS, S)
@@ -98,11 +105,11 @@ def tile_moe_pre_lin_relu2_kernel(tc, xT, w, b, gate, offs, pos1, pos2, out):
             slot0 = e0 * C
             picked = ring.tile([P, PACK, width], F32, name="picked")
             for j in range(PACK):
-                cuts = [0, GATE_FIRST, width] if (g, e0, j) == (0, 0, 0) else [0, width]
-                for c0, c1 in zip(cuts, cuts[1:]):
-                    entries = offs_sb[:, (slot0 + c0) // PER_COL : (slot0 + c1) // PER_COL]
-                    window = x_sb[g, j][:].indirect(entries)
-                    nc.vector.tensor_tensor(picked[:, j, c0:c1], window, gate_sb[:, slot0 + c0 : slot0 + c1], MULT)
+                window = x_sb[g, j][:].indirect(offs_sb[:, slot0 // PER_COL : (slot0 + width) // PER_COL])
+                if (g, e0) == (0, 0):
+                    nc.vector.tensor_copy(picked[:, j, :], window)
+                else:
+                    nc.vector.tensor_tensor(picked[:, j, :], window, gate_sb[:, slot0 : slot0 + width], MULT)
             return picked
 
         spent = []
@@ -124,6 +131,9 @@ def tile_moe_pre_lin_relu2_kernel(tc, xT, w, b, gate, offs, pos1, pos2, out):
                 out=grouped[:].rearrange("p (c i) j -> p c j i", i=RUN),
                 in_=picked[:].rearrange("p j (c i) -> p c j i", i=RUN),
             )
+            quantize_x(grouped, g, e0, n_e)
+
+        def quantize_x(grouped, g, e0, n_e):
             codes, scales = quantize(grouped, f"x_{g}_{e0}")
             for i in range(n_e):
                 x_codes[g, e0 + i] = codes[:, i * C : (i + 1) * C]
@@ -141,6 +151,36 @@ def tile_moe_pre_lin_relu2_kernel(tc, xT, w, b, gate, offs, pos1, pos2, out):
             for i in range(GROUP):
                 w_codes[g, e0 + i] = codes[:, i * N : (i + 1) * N]
                 w_scales[g, e0 + i] = scales[:, i * N : (i + 1) * N]
+
+        def gate_on_scalar(picked, u, tag):
+            pairs = keep.tile([P, EARLY, P, 2], BF16, name="pairs", tag=tag, align_bytes=64)
+            for e0 in range(0, EARLY, 2):
+                turned = psum.tile([P, 2, 2, P], F32, name="turned", tag=f"bank_{4 * u + e0 // 2}")
+                for v in range(2):
+                    for i in range(2):
+                        nc.tensor.transpose(turned[:, i, v, :], picked[:, 2 * u + v, (e0 + i) * C : (e0 + i + 1) * C], ident[:])
+                for i in range(2):
+                    nc.scalar.activation(
+                        out=pairs[:, e0 + i, :, :],
+                        in_=turned[:, i, :, :].rearrange("s v p -> s p v"),
+                        func=COPY,
+                        scale=gate_col[:, e0 + i : e0 + i + 1],
+                    )
+            return pairs[:].rearrange("s e p v -> s (e p v)").bitcast(F32)
+
+        def turn_back(words):
+            grouped = bf16_tile("x_grouped", EARLY_SLOTS, -1)
+            target = grouped[:].rearrange("p c j -> p (c j)").bitcast(F32)
+            for e0 in range(0, EARLY, 2):
+                back = psum.tile([P, 2, 2, C], F32, name="back", tag=f"bank_{e0 // 2}")
+                for u in range(2):
+                    for i in range(2):
+                        nc.tensor.transpose(back[:, i, u, :], words[u][:, (e0 + i) * P : (e0 + i + 1) * P], ident[:])
+                nc.scalar.copy(
+                    out=target[:, 2 * e0 * C : 2 * (e0 + 2) * C].rearrange("p (i s u) -> p i s u", i=2, u=2),
+                    in_=back[:].rearrange("p i u s -> p i s u"),
+                )
+            quantize_x(grouped, 0, 0, EARLY)
 
         def multiply(g, e0, n_e):
             for e in range(e0, e0 + n_e):
@@ -176,11 +216,17 @@ def tile_moe_pre_lin_relu2_kernel(tc, xT, w, b, gate, offs, pos1, pos2, out):
         for u, (g, e0, n_e) in enumerate(steps):
             last = u + 1 == len(steps)
             following = None if last else gather(*steps[u + 1])
+            words = []
             for group in w_groups[done : done + groups_before[u]]:
                 prepare_w(*group)
+                if u == 0:
+                    words.append(gate_on_scalar(picked, len(words), spent[-1] if not words else spent[-2]))
             done = done + groups_before[u]
-            place = -1 if u in (0, first_late) else -2
-            prepare_x(picked, g, e0, n_e, place, nc.vector.tensor_copy if last else nc.scalar.copy)
+            place = -1 if u == first_late else -2
+            if u == 0:
+                turn_back(words)
+            else:
+                prepare_x(picked, g, e0, n_e, place, nc.vector.tensor_copy if last else nc.scalar.copy)
             if u < first_late:
                 multiply(g, e0, n_e)
             elif g == 1:

from contextlib import ExitStack

import concourse.mybir as mybir
from concourse.masks import make_identity

K, T, E, C, N = 1536, 768, 12, 128, 128
S = E * C

FLOPS = 2 * K * N * S
BYTES = 4 * (K * T + E * K * N + N * E + S + N * T) + 2 * 128 * (S + 2 * T) // 16

F32 = mybir.dt.float32
BF16 = mybir.dt.bfloat16
U32 = mybir.dt.uint32
U16 = mybir.dt.uint16
U8 = mybir.dt.uint8
FP8X4 = mybir.dt.float8_e4m3fn_x4
MULT = mybir.AluOpType.mult
ADD = mybir.AluOpType.add
MAX = mybir.AluOpType.max
RELU = mybir.ActivationFunctionType.Relu
SQUARE = mybir.ActivationFunctionType.Square
COPY = mybir.ActivationFunctionType.Copy

P = 128
PACK = 4
K_PASS = P * PACK
PASSES = K // K_PASS
PER_COL = 16
RUN = 4
GROUP = 4
PAIR = 2
BANKS = 8
EARLY = BANKS
EARLY_SLOTS = EARLY * C
WINDOW = EARLY_SLOTS + PER_COL
OUT_SPLIT = 512


def tile_moe_pre_lin_relu2_kernel(tc, xT, w, b, gate, offs, pos1, pos2, out):
    nc = tc.nc
    with ExitStack() as ctx:
        keep = ctx.enter_context(tc.tile_pool(name="keep", bufs=1))
        ring = ctx.enter_context(tc.tile_pool(name="ring", bufs=2))
        psum = ctx.enter_context(tc.psum_pool(name="psum", bufs=1))

        offs_sb = keep.tile([P, S // PER_COL], U16, name="offs_sb")
        pos1_sb = keep.tile([P, T // PER_COL], U16, name="pos1_sb")
        pos2_sb = keep.tile([P, T // PER_COL], U16, name="pos2_sb")
        b_sb = keep.tile([P, E], F32, name="b_sb")
        x_sb = {(g, j): keep.tile([P, WINDOW], F32, name=f"x_{g}_{j}") for g in range(PASSES) for j in range(PACK)}
        gate_sb = keep.tile([P, S], F32, name="gate_sb")
        w_sb = {
            (g, e0): keep.tile([P, PAIR, PACK * N], F32, name=f"w_{g}_{e0}", tag=f"stage_{g}_{e0}", align_bytes=64)
            for g in range(PASSES)
            for e0 in range(0, E, PAIR)
        }
        y = keep.tile([P, S], F32, name="y")

        late = E - EARLY
        steps = [(g, 0, EARLY) for g in range(PASSES)] + [(g, EARLY, late) for g in range(PASSES - 1)]
        steps = steps + [(PASSES - 1, EARLY, 2), (PASSES - 1, EARLY + 2, 1), (PASSES - 1, EARLY + 3, 1)]
        w_groups = [(g, e0) for g in range(PASSES) for e0 in range(0, EARLY, GROUP)] + [(g, EARLY) for g in range(PASSES)]

        def load_x(g, j):
            rows = xT[g * K_PASS : (g + 1) * K_PASS, :].rearrange("(p j) t -> p j t", j=PACK)
            nc.sync.dma_start(out=x_sb[g, j][:, 0:T], in_=rows[:, j, :])

        def load_gate(c0, c1):
            nc.sync.dma_start(out=gate_sb[:, c0:c1], in_=gate[0:P, c0:c1])

        def load_w(g, e0):
            src = w[e0 : e0 + PAIR, g * K_PASS : (g + 1) * K_PASS, :]
            nc.sync.dma_start(out=w_sb[g, e0][:], in_=src.rearrange("e (p j) n -> p e (j n)", j=PACK))

        ident = keep.tile([P, P], F32, name="ident")
        make_identity(nc, ident[:])
        gate_col = keep.tile([P, EARLY], F32, name="gate_col")
        for window in x_sb.values():
            nc.gpsimd.memset(window[:, T:WINDOW], 0.0)

        nc.sync.dma_start(offs_sb[:], offs)
        load_x(0, 0)
        w_pairs = [(g, e0 + i) for g, e0 in w_groups for i in range(0, GROUP, PAIR)]
        later_x = list(x_sb)[1:]
        for window, pair in zip(later_x, w_pairs):
            if window == (0, 2):
                with nc.allow_non_contiguous_dma(reason="one gate value a partition"):
                    nc.sync.dma_start(out=gate_col[:], in_=gate[0, 0:EARLY_SLOTS].rearrange("(e p) -> p e", p=P))
            if window == (1, 0):
                load_gate(0, EARLY_SLOTS)
            load_x(*window)
            load_w(*pair)
        load_gate(EARLY_SLOTS, S)
        nc.sync.dma_start(out=b_sb[:], in_=b)
        for pair in w_pairs[len(later_x) :]:
            load_w(*pair)
        nc.sync.dma_start(pos1_sb[:], pos1)
        nc.sync.dma_start(pos2_sb[:], pos2)

        x_codes, x_scales, w_codes, w_scales, acc = {}, {}, {}, {}, {}

        def gather(g, e0, n_e):
            width = n_e * C
            slot0 = e0 * C
            picked = ring.tile([P, PACK, width], F32, name="picked")
            for j in range(PACK):
                window = x_sb[g, j][:].indirect(offs_sb[:, slot0 // PER_COL : (slot0 + width) // PER_COL])
                if (g, e0) == (0, 0):
                    nc.vector.tensor_copy(picked[:, j, :], window)
                else:
                    nc.vector.tensor_tensor(picked[:, j, :], window, gate_sb[:, slot0 : slot0 + width], MULT)
            return picked

        spent = []

        def bf16_tile(name, width, place):
            tag = spent.pop(place) if spent else name
            return keep.tile([P, width, PACK], BF16, name=name, tag=tag, align_bytes=64)

        def quantize(grouped, name):
            width = grouped.shape[1]
            codes = keep.tile([P, width], U32, name=f"{name}_codes", align_bytes=64)
            scales = keep.tile([P, width], U8, name=f"{name}_scales", align_bytes=64)
            nc.vector.quantize_mx(out=codes[:].bitcast(FP8X4), scales=scales[:], in_=grouped[:].rearrange("p c j -> p (c j)"))
            return codes, scales

        def prepare_x(picked, g, e0, n_e, place, copy):
            grouped = bf16_tile("x_grouped", n_e * C, place)
            copy(
                out=grouped[:].rearrange("p (c i) j -> p c j i", i=RUN),
                in_=picked[:].rearrange("p j (c i) -> p c j i", i=RUN),
            )
            quantize_x(grouped, g, e0, n_e)

        def quantize_x(grouped, g, e0, n_e):
            codes, scales = quantize(grouped, f"x_{g}_{e0}")
            for i in range(n_e):
                x_codes[g, e0 + i] = codes[:, i * C : (i + 1) * C]
                x_scales[g, e0 + i] = scales[:, i * C : (i + 1) * C]

        def prepare_w(g, e0):
            grouped = bf16_tile(f"w_grouped_{g}_{e0}", GROUP * N, 0)
            for i in range(0, GROUP, PAIR):
                nc.scalar.copy(
                    out=grouped[:, i * N : (i + PAIR) * N, :].rearrange("p (e c i) j -> p e c j i", e=PAIR, i=RUN),
                    in_=w_sb[g, e0 + i][:].rearrange("p e (j c i) -> p e c j i", j=PACK, i=RUN),
                )
                spent.append(f"stage_{g}_{e0 + i}")
            codes, scales = quantize(grouped, f"w_{g}_{e0}")
            for i in range(GROUP):
                w_codes[g, e0 + i] = codes[:, i * N : (i + 1) * N]
                w_scales[g, e0 + i] = scales[:, i * N : (i + 1) * N]

        def gate_on_scalar(picked, u, tag):
            pairs = keep.tile([P, EARLY, P, 2], BF16, name="pairs", tag=tag, align_bytes=64)
            for e0 in range(0, EARLY, 2):
                turned = psum.tile([P, 2, 2, P], F32, name="turned", tag=f"bank_{4 * u + e0 // 2}")
                for v in range(2):
                    for i in range(2):
                        nc.tensor.transpose(turned[:, i, v, :], picked[:, 2 * u + v, (e0 + i) * C : (e0 + i + 1) * C], ident[:])
                for i in range(2):
                    nc.scalar.activation(
                        out=pairs[:, e0 + i, :, :],
                        in_=turned[:, i, :, :].rearrange("s v p -> s p v"),
                        func=COPY,
                        scale=gate_col[:, e0 + i : e0 + i + 1],
                    )
            return pairs[:].rearrange("s e p v -> s (e p v)").bitcast(F32)

        def turn_back(words):
            grouped = bf16_tile("x_grouped", EARLY_SLOTS, -1)
            target = grouped[:].rearrange("p c j -> p (c j)").bitcast(F32)
            for e0 in range(0, EARLY, 2):
                back = psum.tile([P, 2, 2, C], F32, name="back", tag=f"bank_{e0 // 2}")
                for u in range(2):
                    for i in range(2):
                        nc.tensor.transpose(back[:, i, u, :], words[u][:, (e0 + i) * P : (e0 + i + 1) * P], ident[:])
                nc.scalar.copy(
                    out=target[:, 2 * e0 * C : 2 * (e0 + 2) * C].rearrange("p (i s u) -> p i s u", i=2, u=2),
                    in_=back[:].rearrange("p i u s -> p i s u"),
                )
            quantize_x(grouped, 0, 0, EARLY)

        def multiply(g, e0, n_e):
            for e in range(e0, e0 + n_e):
                if g == 0:
                    acc[e] = psum.tile([P, C], F32, name="acc", tag=f"bank_{e % BANKS}")
                nc.tensor.matmul_mx(
                    out=acc[e][:],
                    lhsT=w_codes[g, e].bitcast(FP8X4),
                    lhsT_scale=w_scales[g, e],
                    rhs=x_codes[g, e].bitcast(FP8X4),
                    rhs_scale=x_scales[g, e],
                    start=(g == 0),
                    stop=(g == PASSES - 1),
                )

        def finish(e0, n_e):
            relu = ring.tile([P, n_e * C], F32, name="relu")
            for i in range(n_e):
                e = e0 + i
                nc.scalar.activation(out=relu[:, i * C : (i + 1) * C], in_=acc[e][:], func=RELU, bias=b_sb[:, e : e + 1])
            nc.scalar.activation(out=y[:, e0 * C : (e0 + n_e) * C], in_=relu[:], func=SQUARE)

        def finish_on_vector(e):
            relu = keep.tile([P, C], F32, name="relu_last")
            nc.vector.tensor_scalar(out=relu[:], in0=acc[e][:], scalar1=b_sb[:, e : e + 1], scalar2=0.0, op0=ADD, op1=MAX)
            nc.vector.tensor_tensor(y[:, e * C : (e + 1) * C], relu[:], relu[:], MULT)

        groups_before = [2, 2, 3, 0, 2, 0, 0, 0]
        first_late = PASSES

        done = 0
        picked = gather(*steps[0])
        for u, (g, e0, n_e) in enumerate(steps):
            last = u + 1 == len(steps)
            following = None if last else gather(*steps[u + 1])
            words = []
            for group in w_groups[done : done + groups_before[u]]:
                prepare_w(*group)
                if u == 0:
                    words.append(gate_on_scalar(picked, len(words), spent[-1] if not words else spent[-2]))
            done = done + groups_before[u]
            place = -1 if u == first_late else -2
            if u == 0:
                turn_back(words)
            else:
                prepare_x(picked, g, e0, n_e, place, nc.vector.tensor_copy if last else nc.scalar.copy)
            if u < first_late:
                multiply(g, e0, n_e)
            elif g == 1:
                finish(0, late)
                multiply(0, e0, n_e)
                multiply(1, e0, n_e)
            elif g == PASSES - 1:
                multiply(g, e0, n_e)
                if u + 2 == len(steps):
                    finish(late, EARLY - late)
                    finish(EARLY, late - 1)
                if last:
                    finish_on_vector(e0)
            picked = following

        parts = [(0, OUT_SPLIT), (OUT_SPLIT, T)]
        first = [keep.tile([P, t1 - t0], F32, name=f"first_{t0}") for t0, t1 in parts]
        total = [keep.tile([P, t1 - t0], F32, name=f"total_{t0}") for t0, t1 in parts]
        for h, (t0, t1) in enumerate(parts):
            nc.vector.tensor_copy(first[h][:], y[:].indirect(pos1_sb[:, t0 // PER_COL : t1 // PER_COL]))
        for h, (t0, t1) in enumerate(parts):
            nc.vector.tensor_tensor(total[h][:], y[:].indirect(pos2_sb[:, t0 // PER_COL : t1 // PER_COL]), first[h][:], ADD)
            nc.sync.dma_start(out=out[:, t0:t1], in_=total[h][:])
